import numpy as np
import ml_dtypes


def mxq(x, axis, fmt="e4m3"):
    dtype, down = {"e4m3": (ml_dtypes.float8_e4m3fn, 7), "e5m2": (ml_dtypes.float8_e5m2, 14)}[fmt]
    v = np.moveaxis(np.asarray(x, np.float32).astype(ml_dtypes.bfloat16).astype(np.float64), axis, -1)
    blocks = v.reshape(v.shape[:-1] + (-1, 32))
    amax = np.abs(blocks).max(-1, keepdims=True)
    byte = np.maximum(np.where(amax > 0, np.frexp(amax)[1] - 1 + 127, 0) - down, 1)
    scale = np.exp2(byte - 127.0)
    codes = (blocks / scale).astype(np.float32).astype(dtype).astype(np.float64)
    return np.moveaxis((codes * scale).reshape(v.shape), -1, axis)


WIDE = False


def mx_kscale(k):
    if not WIDE:
        return np.ones(k)
    levels = np.array([10, -10, 5, -5, 0])
    if k % 512:
        return np.exp2(np.random.permutation(np.resize(levels, k // 32))).repeat(32)
    a = np.empty((k // 512, 16))
    for p in range(k // 512):
        a[p, :8] = np.random.permutation(np.resize(levels, 8))
        for g in range(8):
            far = levels[np.abs(levels - a[p, g]) >= 10]
            a[p, g + 8] = far[np.random.randint(len(far))]
    return np.exp2(a.ravel()).repeat(32)


def f64(x):
    return np.asarray(x).astype(np.float64)


def striped(idx):
    return np.tile(idx.reshape(-1, 16).T, (8, 1)).astype(np.uint16)


def unstriped(offs):
    return offs[:16].T.reshape(-1).astype(np.int64)


def striped8(idx):
    return np.concatenate([x.reshape(-1, 16).T for x in idx]).astype(np.uint16)


def runs(offs, k):
    lists = np.stack([offs[16 * r : 16 * r + 16].T.reshape(-1) for r in range(8)]).astype(np.int64)
    return lists[np.arange(k) % 512 // 64]


def pack_weight(w):
    k, n = w.shape
    w = f64(np.asarray(w, np.float32).astype(ml_dtypes.bfloat16)).reshape(k // 32, 32, n)
    amax = np.abs(w).max(1)
    byte = np.clip(np.where(amax > 0, np.frexp(amax)[1] - 1 + 127 - 7, 1), 1, 254)
    scaled = (w * np.exp2(127.0 - byte)[:, None, :]).reshape(k, n).astype(np.float32)
    words = np.ascontiguousarray(scaled.reshape(k // 512, 128, 4, n).transpose(0, 1, 3, 2)).astype(ml_dtypes.float8_e4m3fn).view(np.uint8)
    return words, np.ascontiguousarray(byte.astype(np.uint8).reshape(k // 512, 16, n))


def unpack_weight(words, scales):
    g, p, n, _ = words.shape
    vals = np.ascontiguousarray(words).view(ml_dtypes.float8_e4m3fn).astype(np.float64) * np.repeat(np.exp2(scales.astype(np.float64) - 127.0), 8, axis=1)[..., None]
    return vals.transpose(0, 1, 3, 2).reshape(g * 512, n)

def planes(y):
    n, m = y.shape
    v = y.astype(np.float32).astype(ml_dtypes.bfloat16).astype(np.float64).reshape(n // 32, 32, m)
    top = np.abs(v).max(1)
    byte = np.clip(np.where(top > 0, np.frexp(top)[1] - 1 + 127 - 7, 1), 1, 254)
    codes = (v * np.exp2(127.0 - byte)[:, None, :]).reshape(n, m).astype(np.float32).astype(ml_dtypes.float8_e4m3fn).view(np.uint8)
    words = codes.reshape(n // 512, 128, 4, m).transpose(0, 1, 3, 2)
    return np.ascontiguousarray(words), np.ascontiguousarray(byte.astype(np.uint8).reshape(n // 512, 16, m))


K, T, S, H, C = 512, 2048, 512, 512, 512


def setup_inputs():
    n = np.random.standard_normal
    s = mx_kscale(K)[:, None]
    packed_xT = pack_weight(n((K, T)) * s)
    packed_w1 = pack_weight(n((K, H)) / np.sqrt(K) / s)
    return {
        "x_words": packed_xT[0],
        "x_scales": packed_xT[1],
        "w1_words": packed_w1[0],
        "w1_scales": packed_w1[1],
        "gs": (np.random.uniform(0.5, 1.5, (K, 1)) / s).astype(np.float32),
        "offs": striped(np.random.permutation(T)[:S]),
        "n1": striped8(np.stack([np.random.permutation(S) for _ in range(8)])),
        "n2": striped8(np.stack([np.random.permutation(S) for _ in range(8)])),
        "cand": striped(np.random.permutation(T)[:C]),
        "n3": striped8(np.stack([np.random.permutation(S) for _ in range(8)])),
        "n4": striped8(np.stack([np.random.permutation(S) for _ in range(8)])),
        "n5": striped8(np.stack([np.random.permutation(S) for _ in range(8)])),
    }


def reference(x_words, x_scales, w1_words, w1_scales, gs, offs, n1, n2, cand, n3, n4, n5):
    x_cand = unpack_weight(x_words, x_scales)[:, unstriped(cand)]
    xq = unpack_weight(x_words, x_scales)[:, unstriped(offs)]
    y = unpack_weight(w1_words, w1_scales).T @ xq
    ex = np.exp(y)
    z = f64(gs) * (np.log(ex + ex[np.arange(H)[:, None], runs(n1, H)]) - (y[np.arange(H)[:, None], runs(n2, H)]))
    s = 0.0625 * ((x_cand.T @ mxq(z, 0, "e4m3")))
    out_0 = np.maximum(s, s[np.arange(C)[:, None], runs(n3, C)]) - (np.maximum(s[np.arange(C)[:, None], runs(n4, C)], s[np.arange(C)[:, None], runs(n5, C)]))
    return (out_0,) + planes(out_0)

@@ -1,0 +1,200 @@
+from contextlib import ExitStack
+
+import concourse.mybir as mybir
+
+K, T, S, H, C = 512, 2048, 512, 512, 512
+FLOPS = 2 * K * H * S + 2 * K * C * S
+
+F32 = mybir.dt.float32
+BF16 = mybir.dt.bfloat16
+I32 = mybir.dt.int32
+U32 = mybir.dt.uint32
+U16 = mybir.dt.uint16
+U8 = mybir.dt.uint8
+FP8X4 = mybir.dt.float8_e4m3fn_x4
+ACT = mybir.ActivationFunctionType
+ALU = mybir.AluOpType
+
+P = 128
+PACK = 4
+HALF = S // 2
+STRIPE = 16
+OUT_CHUNKS = ((0, 256), (256, 128), (384, 128))
+
+
+def tile_picked_candlsemix_none_po_kernel(tc, x_words, x_scales, w1_words, w1_scales, gs, offs, n1, n2, cand, n3, n4, n5, out_0, out_1, out_2):
+    nc = tc.nc
+    tiles = range(PACK)
+    halves = range(2)
+
+    with ExitStack() as ctx:
+        held = ctx.enter_context(tc.tile_pool(name="held", bufs=1))
+        psum = ctx.enter_context(tc.psum_pool(name="psum", bufs=1))
+
+        def sb(name, shape, dtype):
+            return held.tile(shape, dtype, name=name, align_bytes=64)
+
+        def load_list(name, src):
+            lst = held.tile([P, S // STRIPE], U16, name=name)
+            nc.sync.dma_start(lst[:], src)
+            return lst
+
+        def entries(lst, start, count):
+            return lst[:, start // STRIPE : (start + count) // STRIPE]
+
+        def load_scales(queue, plane, src):
+            for q in range(4):
+                queue.dma_start(plane[32 * q : 32 * q + 4, :].bitcast(I32), src[0, 4 * q : 4 * q + 4, :].bitcast(I32))
+
+        def as_words(src):
+            return src[0].rearrange("p n t -> p (n t)").bitcast(I32)
+
+        def dealt(ap):
+            return ap.rearrange("p (t m) -> p m t", t=PACK)
+
+        def in_order(ap):
+            return ap.rearrange("p (m t) -> p m t", t=PACK)
+
+        def interleave(copy, dst, src):
+            copy(dst.rearrange("p (c i) t -> p c t i", i=4), src.rearrange("p t (c i) -> p c t i", i=4))
+
+        xs = sb("xs", [P, T], U8)
+        ws = sb("ws", [P, H], U8)
+        nc.vector.memset(xs[:].bitcast(I32), 0)
+        nc.vector.memset(ws[:].bitcast(I32), 0)
+        offs_l = load_list("offs_l", offs)
+        cand_l = load_list("cand_l", cand)
+        ww = sb("ww", [P, H], I32)
+        nc.sync.dma_start(ww[:], as_words(w1_words))
+        load_scales(nc.sync, xs, x_scales)
+        xw = sb("xw", [P, T], I32)
+        nc.sync.dma_start(xw[:], as_words(x_words))
+        load_scales(nc.sync, ws, w1_scales)
+        n1_l = load_list("n1_l", n1)
+        gain = sb("gain", [P, PACK], F32)
+        nc.sync.dma_start(gain[:], gs.rearrange("(p t) o -> p (t o)", t=PACK))
+        n2_l = load_list("n2_l", n2)
+        n3_l = load_list("n3_l", n3)
+        n4_l = load_list("n4_l", n4)
+        n5_l = load_list("n5_l", n5)
+
+        tok_s = sb("tok_s", [P, S], U8)
+        nc.vector.tensor_copy(tok_s[:], xs[:].indirect(offs_l[:]))
+        w_w = sb("w_w", [P, H], I32)
+        nc.vector.tensor_copy(dealt(w_w[:]), in_order(ww[:]))
+        cand_s_listed = sb("cand_s_listed", [P, C], U8)
+        nc.vector.tensor_copy(cand_s_listed[:], xs[:].indirect(cand_l[:]))
+        w_s = sb("w_s", [P, H], U8)
+        nc.vector.tensor_copy(dealt(w_s[:]), in_order(ws[:]))
+        tok_w = sb("tok_w", [P, S], U32)
+        nc.vector.tensor_copy(tok_w[:], xw[:].bitcast(U32).indirect(offs_l[:]))
+        cand_w = held.tile([P, C], U32, name="cand_w", tag="ws", align_bytes=64)
+        nc.vector.tensor_copy(dealt(cand_w[:]), xw[:].bitcast(U32).indirect(cand_l[:]))
+        cand_s = sb("cand_s", [P, C], U8)
+        nc.vector.tensor_copy(dealt(cand_s[:]), in_order(cand_s_listed[:]))
+
+        y_ps = [psum.tile([P, S], F32, name=f"y_ps{t}", tag=f"bank{t}") for t in tiles]
+        for t in tiles:
+            rows = slice(t * P, (t + 1) * P)
+            nc.tensor.matmul_mx(out=y_ps[t][:], lhsT=w_w[:, rows].bitcast(FP8X4), lhsT_scale=w_s[:, rows],
+                                rhs=tok_w[:].bitcast(FP8X4), rhs_scale=tok_s[:], start=True, stop=True)
+
+        ex_win = [sb(f"ex_win{t}", [P, S], F32) for t in tiles]
+        ex = [sb(f"ex{t}", [P, S], F32) for t in tiles]
+        gy_win = [sb(f"gy_win{t}", [P, S], F32) for t in tiles]
+        total = [sb(f"total{t}", [P, S], F32) for t in tiles]
+        lse = [sb(f"lse{t}", [P, S], F32) for t in tiles]
+        gy2 = [sb(f"gy2_{t}", [P, S], F32) for t in tiles]
+        for t in tiles:
+            nc.scalar.activation(ex_win[t][:], y_ps[t][:], ACT.Exp)
+            nc.scalar.activation(ex[t][:], y_ps[t][:], ACT.Exp)
+        for t in tiles:
+            for h in halves:
+                cols = slice(h * HALF, (h + 1) * HALF)
+                nc.vector.tensor_tensor(total[t][:, cols], ex_win[t][:].indirect(entries(n1_l, h * HALF, HALF)), ex[t][:, cols], ALU.add)
+        for t in tiles:
+            nc.scalar.activation(gy_win[t][:], y_ps[t][:], ACT.Copy, scale=gain[:, t : t + 1])
+        for t in tiles:
+            nc.scalar.activation(lse[t][:], total[t][:], ACT.Ln)
+        for h in halves:
+            for t in tiles:
+                cols = slice(h * HALF, (h + 1) * HALF)
+                nc.vector.tensor_copy(gy2[t][:, cols], gy_win[t][:].indirect(entries(n2_l, h * HALF, HALF)))
+
+        z_rows = [sb(f"z_rows{h}", [P, PACK, HALF], BF16) for h in halves]
+        z_quad = [sb(f"z_quad{h}", [P, HALF, PACK], BF16) for h in halves]
+        z_w = [sb(f"z_w{h}", [P, HALF], U32) for h in halves]
+        z_s = [sb(f"z_s{h}", [P, HALF], U8) for h in halves]
+        for h in halves:
+            cols = slice(h * HALF, (h + 1) * HALF)
+            for t in tiles:
+                nc.vector.scalar_tensor_tensor(z_rows[h][:, t, :], lse[t][:, cols], gain[:, t : t + 1], gy2[t][:, cols], ALU.mult, ALU.subtract)
+        interleave(nc.scalar.copy, z_quad[0][:], z_rows[0][:])
+        interleave(nc.vector.tensor_copy, z_quad[1][:], z_rows[1][:])
+
+        s_ps = [[psum.tile([P, HALF], F32, name=f"s_ps{h}_{t}", tag=f"bank{4 * (1 - h) + t}") for t in tiles] for h in halves]
+        neg_s = [sb(f"neg_s{t}", [P, S], F32) for t in tiles]
+        for h in halves:
+            nc.vector.quantize_mx(out=z_w[h][:].bitcast(FP8X4), scales=z_s[h][:], in_=z_quad[h][:].rearrange("p j t -> p (j t)"))
+            for t in tiles:
+                rows = slice(t * P, (t + 1) * P)
+                nc.tensor.matmul_mx(out=s_ps[h][t][:], lhsT=cand_w[:, rows].bitcast(FP8X4), lhsT_scale=cand_s[:, rows],
+                                    rhs=z_w[h][:].bitcast(FP8X4), rhs_scale=z_s[h][:], start=True, stop=True)
+            for t in tiles:
+                nc.scalar.activation(neg_s[t][:, h * HALF : (h + 1) * HALF], s_ps[h][t][:], ACT.Copy, scale=-0.0625)
+
+        out_rows = out_0.rearrange("(p t) j -> p t j", t=PACK)
+        o_w = sb("o_w", [P, S], U32)
+        o_s = sb("o_s", [P, S], U8)
+        neg3, neg_top, less4, less5, res, res_quad = {}, {}, {}, {}, {}, {}
+
+        def fetch3(c, t):
+            start, width = OUT_CHUNKS[c]
+            if t == 0:
+                neg3[c] = sb(f"neg3_{c}", [P, PACK, width], F32)
+            nc.vector.tensor_copy(neg3[c][:, t, :], neg_s[t][:].indirect(entries(n3_l, start, width)))
+
+        def combine(c):
+            start, width = OUT_CHUNKS[c]
+            neg_top[c] = sb(f"neg_top{c}", [P, PACK, width], F32)
+            less4[c] = sb(f"less4_{c}", [P, PACK, width], F32)
+            less5[c] = sb(f"less5_{c}", [P, PACK, width], F32)
+            within = slice(start % HALF, start % HALF + width)
+            for t in tiles:
+                nc.vector.scalar_tensor_tensor(neg_top[c][:, t, :], s_ps[start // HALF][t][:, within], -0.0625, neg3[c][:, t, :], ALU.mult, ALU.min)
+            for t in tiles:
+                nc.vector.tensor_tensor(less4[c][:, t, :], neg_s[t][:].indirect(entries(n4_l, start, width)), neg_top[c][:, t, :], ALU.subtract)
+            for t in tiles:
+                nc.vector.tensor_tensor(less5[c][:, t, :], neg_s[t][:].indirect(entries(n5_l, start, width)), neg_top[c][:, t, :], ALU.subtract)
+
+        def finish(c):
+            start, width = OUT_CHUNKS[c]
+            res[c] = sb(f"res{c}", [P, PACK, width], F32)
+            nc.vector.tensor_tensor(res[c][:], less4[c][:], less5[c][:], ALU.min)
+            nc.sync.dma_start(out_rows[:, :, start : start + width], res[c][:])
+            res_quad[c] = sb(f"res_quad{c}", [P, width, PACK], BF16)
+            last = c == len(OUT_CHUNKS) - 1
+            interleave(nc.vector.tensor_copy if last else nc.scalar.copy, res_quad[c][:], res[c][:])
+
+        def quantize_out(c):
+            start, width = OUT_CHUNKS[c]
+            cols = slice(start, start + width)
+            nc.vector.quantize_mx(out=o_w[:, cols].bitcast(FP8X4), scales=o_s[:, cols], in_=res_quad[c][:].rearrange("p j t -> p (j t)"))
+            nc.sync.dma_start(as_words(out_1)[:, cols], o_w[:, cols].bitcast(I32))
+
+        for t in tiles:
+            fetch3(0, t)
+        for c in range(len(OUT_CHUNKS)):
+            combine(c)
+            if c > 0:
+                quantize_out(c - 1)
+            if c + 1 < len(OUT_CHUNKS):
+                fetch3(c + 1, 0)
+            finish(c)
+            if c + 1 < len(OUT_CHUNKS):
+                for t in range(1, PACK):
+                    fetch3(c + 1, t)
+        quantize_out(len(OUT_CHUNKS) - 1)
+        for q in range(4):
+            queue = nc.scalar if q % 2 == 0 else nc.sync
+            queue.dma_start(out_2[0, 4 * q : 4 * q + 4, :].bitcast(I32), o_s[32 * q : 32 * q + 4, :].bitcast(I32))

@@ -19,7 +19,7 @@ P = 128
 PACK = 4
 HALF = S // 2
 STRIPE = 16
-OUT_CHUNKS = ((0, 256), (256, 128), (384, 128))
+WIDE = 2 * S
 
 
 def tile_picked_candlsemix_none_po_kernel(tc, x_words, x_scales, w1_words, w1_scales, gs, offs, n1, n2, cand, n3, n4, n5, out_0, out_1, out_2):
@@ -55,12 +55,18 @@ def tile_picked_candlsemix_none_po_kernel(tc, x_words, x_scales, w1_words, w1_sc
         def in_order(ap):
             return ap.rearrange("p (m t) -> p m t", t=PACK)
 
+        def by_tile(ap):
+            return ap.rearrange("p (t m) -> p t m", t=PACK)
+
+        def strided(ap):
+            return ap.rearrange("p (m t) -> p t m", t=PACK)
+
         def interleave(copy, dst, src):
             copy(dst.rearrange("p (c i) t -> p c t i", i=4), src.rearrange("p t (c i) -> p c t i", i=4))
 
         xs = sb("xs", [P, T], U8)
         ws = sb("ws", [P, H], U8)
-        nc.vector.memset(xs[:].bitcast(I32), 0)
+        nc.gpsimd.memset(xs[:].bitcast(I32), 0)
         nc.vector.memset(ws[:].bitcast(I32), 0)
         offs_l = load_list("offs_l", offs)
         cand_l = load_list("cand_l", cand)
@@ -78,20 +84,23 @@ def tile_picked_candlsemix_none_po_kernel(tc, x_words, x_scales, w1_words, w1_sc
         n4_l = load_list("n4_l", n4)
         n5_l = load_list("n5_l", n5)
 
+        win = [sb(f"win{t}", [P, WIDE], F32) for t in tiles]
+        for t in tiles:
+            nc.vector.memset(win[t][:, S:], 0.0)
+        half_cols = [slice(h * HALF, (h + 1) * HALF) for h in halves]
+
         tok_s = sb("tok_s", [P, S], U8)
         nc.vector.tensor_copy(tok_s[:], xs[:].indirect(offs_l[:]))
         w_w = sb("w_w", [P, H], I32)
-        nc.vector.tensor_copy(dealt(w_w[:]), in_order(ww[:]))
+        nc.gpsimd.tensor_copy(by_tile(w_w[:]), strided(ww[:]))
         cand_s_listed = sb("cand_s_listed", [P, C], U8)
         nc.vector.tensor_copy(cand_s_listed[:], xs[:].indirect(cand_l[:]))
         w_s = sb("w_s", [P, H], U8)
-        nc.vector.tensor_copy(dealt(w_s[:]), in_order(ws[:]))
+        nc.gpsimd.tensor_copy(by_tile(w_s[:]), strided(ws[:]))
         tok_w = sb("tok_w", [P, S], U32)
         nc.vector.tensor_copy(tok_w[:], xw[:].bitcast(U32).indirect(offs_l[:]))
-        cand_w = held.tile([P, C], U32, name="cand_w", tag="ws", align_bytes=64)
+        cand_w = sb("cand_w", [P, C], U32)
         nc.vector.tensor_copy(dealt(cand_w[:]), xw[:].bitcast(U32).indirect(cand_l[:]))
-        cand_s = sb("cand_s", [P, C], U8)
-        nc.vector.tensor_copy(dealt(cand_s[:]), in_order(cand_s_listed[:]))
 
         y_ps = [psum.tile([P, S], F32, name=f"y_ps{t}", tag=f"bank{t}") for t in tiles]
         for t in tiles:
@@ -99,102 +108,114 @@ def tile_picked_candlsemix_none_po_kernel(tc, x_words, x_scales, w1_words, w1_sc
             nc.tensor.matmul_mx(out=y_ps[t][:], lhsT=w_w[:, rows].bitcast(FP8X4), lhsT_scale=w_s[:, rows],
                                 rhs=tok_w[:].bitcast(FP8X4), rhs_scale=tok_s[:], start=True, stop=True)
 
-        ex_win = [sb(f"ex_win{t}", [P, S], F32) for t in tiles]
-        ex = [sb(f"ex{t}", [P, S], F32) for t in tiles]
-        gy_win = [sb(f"gy_win{t}", [P, S], F32) for t in tiles]
+        cand_s_first = sb("cand_s_first", [P, P], U8)
+        nc.vector.tensor_copy(cand_s_first[:], in_order(cand_s_listed[:])[:, :, 0])
+
+        y_win = [sb(f"y_win{t}", [P, WIDE], F32) for t in tiles]
         total = [sb(f"total{t}", [P, S], F32) for t in tiles]
         lse = [sb(f"lse{t}", [P, S], F32) for t in tiles]
-        gy2 = [sb(f"gy2_{t}", [P, S], F32) for t in tiles]
+        diff = [sb(f"diff{t}", [P, S], F32) for t in tiles]
+        nc.vector.tensor_scalar(y_win[0][:, :S], y_ps[0][:], -1.0, None, ALU.mult)
         for t in tiles:
-            nc.scalar.activation(ex_win[t][:], y_ps[t][:], ACT.Exp)
-            nc.scalar.activation(ex[t][:], y_ps[t][:], ACT.Exp)
+            nc.scalar.activation(win[t][:, :S], y_ps[t][:], ACT.Exp)
+            nc.scalar.activation(y_win[t][:, S:], y_ps[t][:], ACT.Exp)
         for t in tiles:
-            for h in halves:
-                cols = slice(h * HALF, (h + 1) * HALF)
-                nc.vector.tensor_tensor(total[t][:, cols], ex_win[t][:].indirect(entries(n1_l, h * HALF, HALF)), ex[t][:, cols], ALU.add)
-        for t in tiles:
-            nc.scalar.activation(gy_win[t][:], y_ps[t][:], ACT.Copy, scale=gain[:, t : t + 1])
+            nc.vector.tensor_tensor(total[t][:], win[t][:].indirect(n1_l[:]), y_win[t][:, S:], ALU.add)
         for t in tiles:
             nc.scalar.activation(lse[t][:], total[t][:], ACT.Ln)
-        for h in halves:
-            for t in tiles:
-                cols = slice(h * HALF, (h + 1) * HALF)
-                nc.vector.tensor_copy(gy2[t][:, cols], gy_win[t][:].indirect(entries(n2_l, h * HALF, HALF)))
+            if t > 0:
+                nc.scalar.activation(y_win[t][:, :S], y_ps[t][:], ACT.Copy, scale=-1.0)
 
-        z_rows = [sb(f"z_rows{h}", [P, PACK, HALF], BF16) for h in halves]
+        z_rows = sb("z_rows", [P, 2, PACK, HALF], BF16)
         z_quad = [sb(f"z_quad{h}", [P, HALF, PACK], BF16) for h in halves]
-        z_w = [sb(f"z_w{h}", [P, HALF], U32) for h in halves]
-        z_s = [sb(f"z_s{h}", [P, HALF], U8) for h in halves]
+        z_w = sb("z_w", [P, S], U32)
+        z_s = sb("z_s", [P, S], U8)
+        last = PACK - 1
+        for t in range(last):
+            nc.vector.tensor_tensor(diff[t][:], y_win[t][:].indirect(n2_l[:]), lse[t][:], ALU.add)
+            nc.scalar.activation(z_rows[:, :, t, :], diff[t][:].rearrange("p (h j) -> p h j", h=2), ACT.Copy, scale=gain[:, t : t + 1])
         for h in halves:
-            cols = slice(h * HALF, (h + 1) * HALF)
-            for t in tiles:
-                nc.vector.scalar_tensor_tensor(z_rows[h][:, t, :], lse[t][:, cols], gain[:, t : t + 1], gy2[t][:, cols], ALU.mult, ALU.subtract)
-        interleave(nc.scalar.copy, z_quad[0][:], z_rows[0][:])
-        interleave(nc.vector.tensor_copy, z_quad[1][:], z_rows[1][:])
+            nc.vector.tensor_tensor(diff[last][:, half_cols[h]], y_win[last][:].indirect(entries(n2_l, h * HALF, HALF)), lse[last][:, half_cols[h]], ALU.add)
+            nc.vector.tensor_scalar(z_rows[:, h, last, :], diff[last][:, half_cols[h]], gain[:, last : last + 1], None, ALU.mult)
+        interleave(nc.scalar.copy, z_quad[0][:], z_rows[:, 0])
+        interleave(nc.vector.tensor_copy, z_quad[1][:], z_rows[:, 1])
 
-        s_ps = [[psum.tile([P, HALF], F32, name=f"s_ps{h}_{t}", tag=f"bank{4 * (1 - h) + t}") for t in tiles] for h in halves]
-        neg_s = [sb(f"neg_s{t}", [P, S], F32) for t in tiles]
+        def score(t, scale, bank, cols):
+            rows = slice(t * P, (t + 1) * P)
+            nc.tensor.matmul_mx(out=bank[:], lhsT=cand_w[:, rows].bitcast(FP8X4), lhsT_scale=scale,
+                                rhs=z_w[:, cols].bitcast(FP8X4), rhs_scale=z_s[:, cols], start=True, stop=True)
+            nc.scalar.activation(win[t][:, cols], bank[:], ACT.Copy, scale=-0.0625)
+
+        s_parts = {}
         for h in halves:
-            nc.vector.quantize_mx(out=z_w[h][:].bitcast(FP8X4), scales=z_s[h][:], in_=z_quad[h][:].rearrange("p j t -> p (j t)"))
-            for t in tiles:
-                rows = slice(t * P, (t + 1) * P)
-                nc.tensor.matmul_mx(out=s_ps[h][t][:], lhsT=cand_w[:, rows].bitcast(FP8X4), lhsT_scale=cand_s[:, rows],
-                                    rhs=z_w[h][:].bitcast(FP8X4), rhs_scale=z_s[h][:], start=True, stop=True)
-            for t in tiles:
-                nc.scalar.activation(neg_s[t][:, h * HALF : (h + 1) * HALF], s_ps[h][t][:], ACT.Copy, scale=-0.0625)
+            nc.vector.quantize_mx(out=z_w[:, half_cols[h]].bitcast(FP8X4), scales=z_s[:, half_cols[h]], in_=z_quad[h][:].rearrange("p j t -> p (j t)"))
+            s_parts[0, h] = psum.tile([P, HALF], F32, name=f"s_ps0_{h}", tag=f"bank{4 + h}")
+            score(0, cand_s_first[:], s_parts[0, h], half_cols[h])
+        cand_s_rest = held.tile([P, last * P], U8, name="cand_s_rest", tag="z_quad1", align_bytes=64)
+        nc.vector.tensor_copy(cand_s_rest[:].rearrange("p (t m) -> p m t", t=last), in_order(cand_s_listed[:])[:, :, 1:])
+        s_ps = {}
+        for t in range(1, PACK):
+            s_ps[t] = psum.tile([P, S], F32, name=f"s_ps{t}", tag=f"bank{(5 + t) % 8}")
+            score(t, cand_s_rest[:, (t - 1) * P : t * P], s_ps[t], slice(0, S))
 
         out_rows = out_0.rearrange("(p t) j -> p t j", t=PACK)
         o_w = sb("o_w", [P, S], U32)
         o_s = sb("o_s", [P, S], U8)
-        neg3, neg_top, less4, less5, res, res_quad = {}, {}, {}, {}, {}, {}
+        neg3 = [sb(f"neg3_{t}", [P, S], F32) for t in tiles]
+        neg_top = [sb(f"neg_top{t}", [P, S], F32) for t in tiles]
+        less4 = [sb(f"less4_{t}", [P, S], F32) for t in tiles]
+        less5 = [sb(f"less5_{t}", [P, S], F32) for t in tiles]
+        res = [sb(f"res{u}", [P, 2, S], F32) for u in range(2)]
+        res_quad = sb("res_quad", [P, S, PACK], BF16)
+        whole = slice(0, S)
 
-        def fetch3(c, t):
-            start, width = OUT_CHUNKS[c]
+        def listed(lst, cols):
+            return entries(lst, cols.start, cols.stop - cols.start)
+
+        def fetch3(t, cols):
+            nc.vector.tensor_copy(neg3[t][:, cols], win[t][:].indirect(listed(n3_l, cols)))
+
+        def top(t, cols):
             if t == 0:
-                neg3[c] = sb(f"neg3_{c}", [P, PACK, width], F32)
-            nc.vector.tensor_copy(neg3[c][:, t, :], neg_s[t][:].indirect(entries(n3_l, start, width)))
+                for h in halves:
+                    nc.vector.scalar_tensor_tensor(neg_top[t][:, half_cols[h]], s_parts[0, h][:], -0.0625, neg3[t][:, half_cols[h]], ALU.mult, ALU.min)
+            else:
+                nc.vector.scalar_tensor_tensor(neg_top[t][:, cols], s_ps[t][:, cols], -0.0625, neg3[t][:, cols], ALU.mult, ALU.min)
 
-        def combine(c):
-            start, width = OUT_CHUNKS[c]
-            neg_top[c] = sb(f"neg_top{c}", [P, PACK, width], F32)
-            less4[c] = sb(f"less4_{c}", [P, PACK, width], F32)
-            less5[c] = sb(f"less5_{c}", [P, PACK, width], F32)
-            within = slice(start % HALF, start % HALF + width)
-            for t in tiles:
-                nc.vector.scalar_tensor_tensor(neg_top[c][:, t, :], s_ps[start // HALF][t][:, within], -0.0625, neg3[c][:, t, :], ALU.mult, ALU.min)
-            for t in tiles:
-                nc.vector.tensor_tensor(less4[c][:, t, :], neg_s[t][:].indirect(entries(n4_l, start, width)), neg_top[c][:, t, :], ALU.subtract)
-            for t in tiles:
-                nc.vector.tensor_tensor(less5[c][:, t, :], neg_s[t][:].indirect(entries(n5_l, start, width)), neg_top[c][:, t, :], ALU.subtract)
+        def fetch45(t, cols):
+            nc.vector.tensor_tensor(less4[t][:, cols], win[t][:].indirect(listed(n4_l, cols)), neg_top[t][:, cols], ALU.subtract)
+            nc.vector.tensor_tensor(less5[t][:, cols], win[t][:].indirect(listed(n5_l, cols)), neg_top[t][:, cols], ALU.subtract)
 
-        def finish(c):
-            start, width = OUT_CHUNKS[c]
-            res[c] = sb(f"res{c}", [P, PACK, width], F32)
-            nc.vector.tensor_tensor(res[c][:], less4[c][:], less5[c][:], ALU.min)
-            nc.sync.dma_start(out_rows[:, :, start : start + width], res[c][:])
-            res_quad[c] = sb(f"res_quad{c}", [P, width, PACK], BF16)
-            last = c == len(OUT_CHUNKS) - 1
-            interleave(nc.vector.tensor_copy if last else nc.scalar.copy, res_quad[c][:], res[c][:])
+        def finish(t, cols):
+            nc.vector.tensor_tensor(res[t // 2][:, t % 2, cols], less4[t][:, cols], less5[t][:, cols], ALU.min)
+            nc.sync.dma_start(out_rows[:, t, cols], res[t // 2][:, t % 2, cols])
 
-        def quantize_out(c):
-            start, width = OUT_CHUNKS[c]
-            cols = slice(start, start + width)
-            nc.vector.quantize_mx(out=o_w[:, cols].bitcast(FP8X4), scales=o_s[:, cols], in_=res_quad[c][:].rearrange("p j t -> p (j t)"))
+        def round_pair(copy, u, cols):
+            interleave(copy, res_quad[:, cols, 2 * u : 2 * u + 2], res[u][:, :, cols])
+
+        def planes(cols):
+            nc.vector.quantize_mx(out=o_w[:, cols].bitcast(FP8X4), scales=o_s[:, cols], in_=res_quad[:, cols, :].rearrange("p j t -> p (j t)"))
             nc.sync.dma_start(as_words(out_1)[:, cols], o_w[:, cols].bitcast(I32))
 
-        for t in tiles:
-            fetch3(0, t)
-        for c in range(len(OUT_CHUNKS)):
-            combine(c)
-            if c > 0:
-                quantize_out(c - 1)
-            if c + 1 < len(OUT_CHUNKS):
-                fetch3(c + 1, 0)
-            finish(c)
-            if c + 1 < len(OUT_CHUNKS):
-                for t in range(1, PACK):
-                    fetch3(c + 1, t)
-        quantize_out(len(OUT_CHUNKS) - 1)
+        steps = [(t, whole) for t in range(last)] + [(last, half_cols[h]) for h in halves]
+        fetch3(*steps[0])
+        fetch3(*steps[1])
+        top(*steps[0])
+        for i, step in enumerate(steps):
+            if i + 1 < len(steps):
+                top(*steps[i + 1])
+            fetch45(*step)
+            if i + 2 < len(steps):
+                fetch3(*steps[i + 2])
+            if i == len(steps) - 1:
+                planes(half_cols[0])
+            finish(*step)
+            if step[0] == 1:
+                round_pair(nc.scalar.copy, 0, whole)
+            if i == last:
+                round_pair(nc.scalar.copy, 1, half_cols[0])
+        round_pair(nc.vector.tensor_copy, 1, half_cols[1])
+        planes(half_cols[1])
         for q in range(4):
             queue = nc.scalar if q % 2 == 0 else nc.sync
             queue.dma_start(out_2[0, 4 * q : 4 * q + 4, :].bitcast(I32), o_s[32 * q : 32 * q + 4, :].bitcast(I32))

@@ -1,6 +1,7 @@
 from contextlib import ExitStack
 
 import concourse.mybir as mybir
+from concourse.masks import make_identity
 
 K, T, S, H, C = 512, 2048, 512, 512, 512
 FLOPS = 2 * K * H * S + 2 * K * C * S
@@ -20,6 +21,7 @@ PACK = 4
 HALF = S // 2
 STRIPE = 16
 WIDE = 2 * S
+TURNED = 2
 
 
 def tile_picked_candlsemix_none_po_kernel(tc, x_words, x_scales, w1_words, w1_scales, gs, offs, n1, n2, cand, n3, n4, n5, out_0, out_1, out_2):
@@ -55,18 +57,25 @@ def tile_picked_candlsemix_none_po_kernel(tc, x_words, x_scales, w1_words, w1_sc
         def in_order(ap):
             return ap.rearrange("p (m t) -> p m t", t=PACK)
 
-        def by_tile(ap):
-            return ap.rearrange("p (t m) -> p t m", t=PACK)
+        def deal_first(name, src, tag):
+            dst = held.tile([P, P], U8, name=name, tag=tag, align_bytes=64)
+            nc.vector.tensor_copy(dst[:], in_order(src[:])[:, :, 0])
+            return dst
 
-        def strided(ap):
-            return ap.rearrange("p (m t) -> p t m", t=PACK)
+        def deal_rest(name, src, tag):
+            dst = held.tile([P, (PACK - 1) * P], U8, name=name, tag=tag, align_bytes=64)
+            nc.vector.tensor_copy(dst[:].rearrange("p (t m) -> p m t", t=PACK - 1), in_order(src[:])[:, :, 1:])
+            return dst
+
+        def tile_scales(first, rest, t):
+            return first[:] if t == 0 else rest[:, (t - 1) * P : t * P]
 
         def interleave(copy, dst, src):
             copy(dst.rearrange("p (c i) t -> p c t i", i=4), src.rearrange("p t (c i) -> p c t i", i=4))
 
         xs = sb("xs", [P, T], U8)
         ws = sb("ws", [P, H], U8)
-        nc.gpsimd.memset(xs[:].bitcast(I32), 0)
+        nc.vector.memset(xs[:].bitcast(I32), 0)
         nc.vector.memset(ws[:].bitcast(I32), 0)
         offs_l = load_list("offs_l", offs)
         cand_l = load_list("cand_l", cand)
@@ -87,50 +96,59 @@ def tile_picked_candlsemix_none_po_kernel(tc, x_words, x_scales, w1_words, w1_sc
         win = [sb(f"win{t}", [P, WIDE], F32) for t in tiles]
         for t in tiles:
             nc.vector.memset(win[t][:, S:], 0.0)
+        ident = sb("ident", [P, P], F32)
+        make_identity(nc, ident[:])
         half_cols = [slice(h * HALF, (h + 1) * HALF) for h in halves]
 
         tok_s = sb("tok_s", [P, S], U8)
         nc.vector.tensor_copy(tok_s[:], xs[:].indirect(offs_l[:]))
         w_w = sb("w_w", [P, H], I32)
-        nc.gpsimd.tensor_copy(by_tile(w_w[:]), strided(ww[:]))
+        nc.vector.tensor_copy(dealt(w_w[:]), in_order(ww[:]))
         cand_s_listed = sb("cand_s_listed", [P, C], U8)
         nc.vector.tensor_copy(cand_s_listed[:], xs[:].indirect(cand_l[:]))
-        w_s = sb("w_s", [P, H], U8)
-        nc.gpsimd.tensor_copy(by_tile(w_s[:]), strided(ws[:]))
         tok_w = sb("tok_w", [P, S], U32)
         nc.vector.tensor_copy(tok_w[:], xw[:].bitcast(U32).indirect(offs_l[:]))
-        cand_w = sb("cand_w", [P, C], U32)
+        w_s_first = deal_first("w_s_first", ws, "w_s_first")
+        w_s_rest = deal_rest("w_s_rest", ws, "w_s_rest")
+        cand_w = held.tile([P, C], U32, name="cand_w", tag="ws", align_bytes=64)
         nc.vector.tensor_copy(dealt(cand_w[:]), xw[:].bitcast(U32).indirect(cand_l[:]))
 
         y_ps = [psum.tile([P, S], F32, name=f"y_ps{t}", tag=f"bank{t}") for t in tiles]
-        for t in tiles:
+        last = PACK - 1
+        for t in (0, last, 1, 2):
             rows = slice(t * P, (t + 1) * P)
-            nc.tensor.matmul_mx(out=y_ps[t][:], lhsT=w_w[:, rows].bitcast(FP8X4), lhsT_scale=w_s[:, rows],
+            nc.tensor.matmul_mx(out=y_ps[t][:], lhsT=w_w[:, rows].bitcast(FP8X4), lhsT_scale=tile_scales(w_s_first, w_s_rest, t),
                                 rhs=tok_w[:].bitcast(FP8X4), rhs_scale=tok_s[:], start=True, stop=True)
 
-        cand_s_first = sb("cand_s_first", [P, P], U8)
-        nc.vector.tensor_copy(cand_s_first[:], in_order(cand_s_listed[:])[:, :, 0])
+        cand_s_first = deal_first("cand_s_first", cand_s_listed, "cand_s_first")
 
         y_win = [sb(f"y_win{t}", [P, WIDE], F32) for t in tiles]
-        total = [sb(f"total{t}", [P, S], F32) for t in tiles]
+        total = [sb(f"total{t}", [P, S], F32)[:] for t in tiles]
         lse = [sb(f"lse{t}", [P, S], F32) for t in tiles]
         diff = [sb(f"diff{t}", [P, S], F32) for t in tiles]
-        nc.vector.tensor_scalar(y_win[0][:, :S], y_ps[0][:], -1.0, None, ALU.mult)
+
+        def negate_on_vector(t):
+            nc.vector.tensor_scalar(y_win[t][:, :S], y_ps[t][:], -1.0, None, ALU.mult)
+
+        negate_on_vector(last)
         for t in tiles:
             nc.scalar.activation(win[t][:, :S], y_ps[t][:], ACT.Exp)
-            nc.scalar.activation(y_win[t][:, S:], y_ps[t][:], ACT.Exp)
+            if t != 1:
+                nc.scalar.activation(y_win[t][:, S:], y_ps[t][:], ACT.Exp)
         for t in tiles:
-            nc.vector.tensor_tensor(total[t][:], win[t][:].indirect(n1_l[:]), y_win[t][:, S:], ALU.add)
+            nc.vector.tensor_tensor(total[t], win[t][:].indirect(n1_l[:]), y_win[t][:, S:], ALU.add)
+            if t == 0:
+                nc.vector.tensor_copy(y_win[1][:, S:], win[1][:, :S])
+                negate_on_vector(0)
         for t in tiles:
-            nc.scalar.activation(lse[t][:], total[t][:], ACT.Ln)
-            if t > 0:
+            if t in (1, 2):
                 nc.scalar.activation(y_win[t][:, :S], y_ps[t][:], ACT.Copy, scale=-1.0)
+            nc.scalar.activation(lse[t][:], total[t], ACT.Ln)
 
         z_rows = sb("z_rows", [P, 2, PACK, HALF], BF16)
         z_quad = [sb(f"z_quad{h}", [P, HALF, PACK], BF16) for h in halves]
         z_w = sb("z_w", [P, S], U32)
         z_s = sb("z_s", [P, S], U8)
-        last = PACK - 1
         for t in range(last):
             nc.vector.tensor_tensor(diff[t][:], y_win[t][:].indirect(n2_l[:]), lse[t][:], ALU.add)
             nc.scalar.activation(z_rows[:, :, t, :], diff[t][:].rearrange("p (h j) -> p h j", h=2), ACT.Copy, scale=gain[:, t : t + 1])
@@ -151,44 +169,25 @@ def tile_picked_candlsemix_none_po_kernel(tc, x_words, x_scales, w1_words, w1_sc
             nc.vector.quantize_mx(out=z_w[:, half_cols[h]].bitcast(FP8X4), scales=z_s[:, half_cols[h]], in_=z_quad[h][:].rearrange("p j t -> p (j t)"))
             s_parts[0, h] = psum.tile([P, HALF], F32, name=f"s_ps0_{h}", tag=f"bank{4 + h}")
             score(0, cand_s_first[:], s_parts[0, h], half_cols[h])
-        cand_s_rest = held.tile([P, last * P], U8, name="cand_s_rest", tag="z_quad1", align_bytes=64)
-        nc.vector.tensor_copy(cand_s_rest[:].rearrange("p (t m) -> p m t", t=last), in_order(cand_s_listed[:])[:, :, 1:])
+        cand_s_rest = deal_rest("cand_s_rest", cand_s_listed, "z_quad1")
         s_ps = {}
+        pos_s = [sb(f"pos_s{t}", [P, S], F32) for t in range(TURNED)]
         for t in range(1, PACK):
             s_ps[t] = psum.tile([P, S], F32, name=f"s_ps{t}", tag=f"bank{(5 + t) % 8}")
+            if t <= TURNED:
+                nc.scalar.activation(pos_s[t - 1][:], win[t - 1][:, :S], ACT.Copy, scale=-1.0)
             score(t, cand_s_rest[:, (t - 1) * P : t * P], s_ps[t], slice(0, S))
 
         out_rows = out_0.rearrange("(p t) j -> p t j", t=PACK)
         o_w = sb("o_w", [P, S], U32)
         o_s = sb("o_s", [P, S], U8)
-        neg3 = [sb(f"neg3_{t}", [P, S], F32) for t in tiles]
-        neg_top = [sb(f"neg_top{t}", [P, S], F32) for t in tiles]
-        less4 = [sb(f"less4_{t}", [P, S], F32) for t in tiles]
-        less5 = [sb(f"less5_{t}", [P, S], F32) for t in tiles]
         res = [sb(f"res{u}", [P, 2, S], F32) for u in range(2)]
         res_quad = sb("res_quad", [P, S, PACK], BF16)
         whole = slice(0, S)
+        blocks = [slice(b * P, (b + 1) * P) for b in range(S // P)]
 
-        def listed(lst, cols):
-            return entries(lst, cols.start, cols.stop - cols.start)
-
-        def fetch3(t, cols):
-            nc.vector.tensor_copy(neg3[t][:, cols], win[t][:].indirect(listed(n3_l, cols)))
-
-        def top(t, cols):
-            if t == 0:
-                for h in halves:
-                    nc.vector.scalar_tensor_tensor(neg_top[t][:, half_cols[h]], s_parts[0, h][:], -0.0625, neg3[t][:, half_cols[h]], ALU.mult, ALU.min)
-            else:
-                nc.vector.scalar_tensor_tensor(neg_top[t][:, cols], s_ps[t][:, cols], -0.0625, neg3[t][:, cols], ALU.mult, ALU.min)
-
-        def fetch45(t, cols):
-            nc.vector.tensor_tensor(less4[t][:, cols], win[t][:].indirect(listed(n4_l, cols)), neg_top[t][:, cols], ALU.subtract)
-            nc.vector.tensor_tensor(less5[t][:, cols], win[t][:].indirect(listed(n5_l, cols)), neg_top[t][:, cols], ALU.subtract)
-
-        def finish(t, cols):
-            nc.vector.tensor_tensor(res[t // 2][:, t % 2, cols], less4[t][:, cols], less5[t][:, cols], ALU.min)
-            nc.sync.dma_start(out_rows[:, t, cols], res[t // 2][:, t % 2, cols])
+        def store(queue, t, cols):
+            queue.dma_start(out_rows[:, t, cols], res[t // 2][:, t % 2, cols])
 
         def round_pair(copy, u, cols):
             interleave(copy, res_quad[:, cols, 2 * u : 2 * u + 2], res[u][:, :, cols])
@@ -197,25 +196,64 @@ def tile_picked_candlsemix_none_po_kernel(tc, x_words, x_scales, w1_words, w1_sc
             nc.vector.quantize_mx(out=o_w[:, cols].bitcast(FP8X4), scales=o_s[:, cols], in_=res_quad[:, cols, :].rearrange("p j t -> p (j t)"))
             nc.sync.dma_start(as_words(out_1)[:, cols], o_w[:, cols].bitcast(I32))
 
-        steps = [(t, whole) for t in range(last)] + [(last, half_cols[h]) for h in halves]
-        fetch3(*steps[0])
-        fetch3(*steps[1])
-        top(*steps[0])
-        for i, step in enumerate(steps):
-            if i + 1 < len(steps):
-                top(*steps[i + 1])
-            fetch45(*step)
-            if i + 2 < len(steps):
-                fetch3(*steps[i + 2])
-            if i == len(steps) - 1:
-                planes(half_cols[0])
-            finish(*step)
-            if step[0] == 1:
-                round_pair(nc.scalar.copy, 0, whole)
-            if i == last:
-                round_pair(nc.scalar.copy, 1, half_cols[0])
-        round_pair(nc.vector.tensor_copy, 1, half_cols[1])
-        planes(half_cols[1])
+        turned = [sb(f"turned{t}", [P, S], F32) for t in range(TURNED)]
+
+        def turn_back(t):
+            back = psum.tile([P, S], F32, name=f"back{t}", tag="bank2")
+            for block in blocks:
+                nc.tensor.transpose(back[:, block], turned[t][:, block], ident[:])
+            nc.scalar.copy(res[t // 2][:, t % 2, :], back[:])
+            store(nc.scalar, t, whole)
+
+        for t in range(TURNED):
+            neg4 = sb(f"neg4_{t}", [P, S], F32)
+            below3 = sb(f"below3_{t}", [P, S], F32)
+            gap = sb(f"gap{t}", [P, S], F32)
+            rise = held.tile([P, S], F32, name=f"rise{t}", tag="rise", align_bytes=64)
+            drop = sb(f"drop{t}", [P, S], F32)
+            nc.vector.tensor_copy(neg4[:], win[t][:].indirect(n4_l[:]))
+            nc.vector.tensor_tensor(below3[:], win[t][:].indirect(n3_l[:]), pos_s[t][:], ALU.add)
+            nc.scalar.activation(rise[:], below3[:], ACT.Relu, scale=-1.0)
+            nc.vector.tensor_tensor(gap[:], win[t][:].indirect(n5_l[:]), neg4[:], ALU.subtract)
+            nc.vector.tensor_scalar(drop[:], gap[:], 0.0, None, ALU.min)
+            if t > 0:
+                turn_back(t - 1)
+            summed = psum.tile([P, S], F32, name=f"summed{t}", tag="bank1")
+            terms = (pos_s[t], neg4, rise, drop)
+            for block in blocks:
+                for i, term in enumerate(terms):
+                    nc.tensor.matmul(summed[:, block], term[:, block], ident[:], is_transpose=True, start=i == 0, stop=i == len(terms) - 1)
+            nc.scalar.copy(turned[t][:], summed[:])
+        turn_back(TURNED - 1)
+        round_pair(nc.scalar.copy, 0, whole)
+
+        direct = range(TURNED, PACK)
+        neg3 = {t: sb(f"neg3_{t}", [P, S], F32) for t in direct}
+        neg_top = {t: sb(f"neg_top{t}", [P, S], F32) for t in direct}
+        less4 = {t: sb(f"less4_{t}", [P, S], F32) for t in direct}
+        less5 = {t: sb(f"less5_{t}", [P, S], F32) for t in direct}
+
+        def finish(t, cols):
+            nc.vector.tensor_tensor(res[1][:, t % 2, cols], less4[t][:, cols], less5[t][:, cols], ALU.min)
+            store(nc.sync, t, cols)
+
+        for t in direct:
+            nc.vector.tensor_copy(neg3[t][:], win[t][:].indirect(n3_l[:]))
+        for t in direct:
+            nc.vector.scalar_tensor_tensor(neg_top[t][:], s_ps[t][:], -0.0625, neg3[t][:], ALU.mult, ALU.min)
+        for lst, less in ((n4_l, less4), (n5_l, less5)):
+            nc.vector.tensor_tensor(less[TURNED][:], win[TURNED][:].indirect(lst[:]), neg_top[TURNED][:], ALU.subtract)
+        nc.vector.tensor_tensor(less4[last][:], win[last][:].indirect(n4_l[:]), neg_top[last][:], ALU.subtract)
+        finish(TURNED, whole)
+        for h in halves:
+            cols = half_cols[h]
+            nc.vector.tensor_tensor(less5[last][:, cols], win[last][:].indirect(entries(n5_l, h * HALF, HALF)), neg_top[last][:, cols], ALU.subtract)
+        for h in halves:
+            finish(last, half_cols[h])
+        for h in halves:
+            round_pair(nc.vector.tensor_copy, 1, half_cols[h])
+        for h in halves:
+            planes(half_cols[h])
         for q in range(4):
             queue = nc.scalar if q % 2 == 0 else nc.sync
             queue.dma_start(out_2[0, 4 * q : 4 * q + 4, :].bitcast(I32), o_s[32 * q : 32 * q + 4, :].bitcast(I32))

@@ -18,38 +18,57 @@ ALU = mybir.AluOpType
 
 P = 128
 PACK = 4
-HALF = S // 2
+QUADRANT = 32
+SCALE_ROWS = 4
 STRIPE = 16
+HALF = S // 2
 WIDE = 2 * S
+RUN = 4
+SCORE_SCALE = 0.0625
 TURNED = 2
 
 
-def tile_picked_candlsemix_none_po_kernel(tc, x_words, x_scales, w1_words, w1_scales, gs, offs, n1, n2, cand, n3, n4, n5, out_0, out_1, out_2):
+def tile_picked_candlsemix_none_po_kernel(
+    tc, x_words, x_scales, w1_words, w1_scales, gs, offs, n1, n2, cand, n3, n4, n5, out_0, out_1, out_2
+):
     nc = tc.nc
     tiles = range(PACK)
     halves = range(2)
+    quadrants = range(P // QUADRANT)
+    last = PACK - 1
+    whole = slice(0, S)
+    half_cols = [slice(h * HALF, (h + 1) * HALF) for h in halves]
 
     with ExitStack() as ctx:
         held = ctx.enter_context(tc.tile_pool(name="held", bufs=1))
         psum = ctx.enter_context(tc.psum_pool(name="psum", bufs=1))
 
-        def sb(name, shape, dtype):
-            return held.tile(shape, dtype, name=name, align_bytes=64)
+        def sb(name, shape, dtype, bytes_of=None):
+            return held.tile(shape, dtype, name=name, tag=bytes_of or name, align_bytes=64)
+
+        def bank(name, number, width):
+            return psum.tile([P, width], F32, name=name, tag=f"bank{number}")
 
         def load_list(name, src):
             lst = held.tile([P, S // STRIPE], U16, name=name)
             nc.sync.dma_start(lst[:], src)
             return lst
 
-        def entries(lst, start, count):
-            return lst[:, start // STRIPE : (start + count) // STRIPE]
+        def half_of(lst, h):
+            return lst[:, h * HALF // STRIPE : (h + 1) * HALF // STRIPE]
 
-        def load_scales(queue, plane, src):
-            for q in range(4):
-                queue.dma_start(plane[32 * q : 32 * q + 4, :].bitcast(I32), src[0, 4 * q : 4 * q + 4, :].bitcast(I32))
+        def live_rows(plane, q):
+            return plane[QUADRANT * q : QUADRANT * q + SCALE_ROWS, :].bitcast(I32)
 
-        def as_words(src):
-            return src[0].rearrange("p n t -> p (n t)").bitcast(I32)
+        def scale_rows(dram, q):
+            return dram[0, SCALE_ROWS * q : SCALE_ROWS * (q + 1), :].bitcast(I32)
+
+        def load_scales(plane, src):
+            for q in quadrants:
+                nc.sync.dma_start(live_rows(plane, q), scale_rows(src, q))
+
+        def as_words(dram):
+            return dram[0].rearrange("p n t -> p (n t)").bitcast(I32)
 
         def dealt(ap):
             return ap.rearrange("p (t m) -> p m t", t=PACK)
@@ -57,34 +76,48 @@ def tile_picked_candlsemix_none_po_kernel(tc, x_words, x_scales, w1_words, w1_sc
         def in_order(ap):
             return ap.rearrange("p (m t) -> p m t", t=PACK)
 
-        def deal_first(name, src, tag):
-            dst = held.tile([P, P], U8, name=name, tag=tag, align_bytes=64)
+        def deal_first(name, src, bytes_of=None):
+            dst = sb(name, [P, P], U8, bytes_of)
             nc.vector.tensor_copy(dst[:], in_order(src[:])[:, :, 0])
             return dst
 
-        def deal_rest(name, src, tag):
-            dst = held.tile([P, (PACK - 1) * P], U8, name=name, tag=tag, align_bytes=64)
-            nc.vector.tensor_copy(dst[:].rearrange("p (t m) -> p m t", t=PACK - 1), in_order(src[:])[:, :, 1:])
+        def deal_rest(name, src, bytes_of=None):
+            dst = sb(name, [P, last * P], U8, bytes_of)
+            nc.vector.tensor_copy(dst[:].rearrange("p (t m) -> p m t", t=last), in_order(src[:])[:, :, 1:])
             return dst
 
-        def tile_scales(first, rest, t):
-            return first[:] if t == 0 else rest[:, (t - 1) * P : t * P]
+        def rest_of(rest, t):
+            return rest[:, (t - 1) * P : t * P]
+
+        def product(dst, words, t, scales, moving_words, moving_scales):
+            nc.tensor.matmul_mx(
+                out=dst[:],
+                lhsT=words[:, t * P : (t + 1) * P].bitcast(FP8X4),
+                lhsT_scale=scales,
+                rhs=moving_words.bitcast(FP8X4),
+                rhs_scale=moving_scales,
+                start=True,
+                stop=True,
+            )
 
         def interleave(copy, dst, src):
-            copy(dst.rearrange("p (c i) t -> p c t i", i=4), src.rearrange("p t (c i) -> p c t i", i=4))
+            copy(dst.rearrange("p (c i) t -> p c t i", i=RUN), src.rearrange("p t (c i) -> p c t i", i=RUN))
 
-        xs = sb("xs", [P, T], U8)
-        ws = sb("ws", [P, H], U8)
-        nc.vector.memset(xs[:].bitcast(I32), 0)
-        nc.vector.memset(ws[:].bitcast(I32), 0)
+        def quantize(words, scales, quad):
+            nc.vector.quantize_mx(out=words.bitcast(FP8X4), scales=scales, in_=quad.rearrange("p j t -> p (j t)"))
+
+        x_plane = sb("x_plane", [P, T], U8)
+        w_plane = sb("w_plane", [P, H], U8)
+        nc.vector.memset(x_plane[:].bitcast(I32), 0)
+        nc.vector.memset(w_plane[:].bitcast(I32), 0)
         offs_l = load_list("offs_l", offs)
         cand_l = load_list("cand_l", cand)
-        ww = sb("ww", [P, H], I32)
-        nc.sync.dma_start(ww[:], as_words(w1_words))
-        load_scales(nc.sync, xs, x_scales)
-        xw = sb("xw", [P, T], I32)
-        nc.sync.dma_start(xw[:], as_words(x_words))
-        load_scales(nc.sync, ws, w1_scales)
+        w_loaded = sb("w_loaded", [P, H], I32)
+        nc.sync.dma_start(w_loaded[:], as_words(w1_words))
+        load_scales(x_plane, x_scales)
+        x_loaded = sb("x_loaded", [P, T], I32)
+        nc.sync.dma_start(x_loaded[:], as_words(x_words))
+        load_scales(w_plane, w1_scales)
         n1_l = load_list("n1_l", n1)
         gain = sb("gain", [P, PACK], F32)
         nc.sync.dma_start(gain[:], gs.rearrange("(p t) o -> p (t o)", t=PACK))
@@ -98,34 +131,31 @@ def tile_picked_candlsemix_none_po_kernel(tc, x_words, x_scales, w1_words, w1_sc
             nc.vector.memset(win[t][:, S:], 0.0)
         ident = sb("ident", [P, P], F32)
         make_identity(nc, ident[:])
-        half_cols = [slice(h * HALF, (h + 1) * HALF) for h in halves]
 
         tok_s = sb("tok_s", [P, S], U8)
-        nc.vector.tensor_copy(tok_s[:], xs[:].indirect(offs_l[:]))
+        nc.vector.tensor_copy(tok_s[:], x_plane[:].indirect(offs_l[:]))
         w_w = sb("w_w", [P, H], I32)
-        nc.vector.tensor_copy(dealt(w_w[:]), in_order(ww[:]))
+        nc.vector.tensor_copy(dealt(w_w[:]), in_order(w_loaded[:]))
         cand_s_listed = sb("cand_s_listed", [P, C], U8)
-        nc.vector.tensor_copy(cand_s_listed[:], xs[:].indirect(cand_l[:]))
+        nc.vector.tensor_copy(cand_s_listed[:], x_plane[:].indirect(cand_l[:]))
         tok_w = sb("tok_w", [P, S], U32)
-        nc.vector.tensor_copy(tok_w[:], xw[:].bitcast(U32).indirect(offs_l[:]))
-        w_s_first = deal_first("w_s_first", ws, "w_s_first")
-        w_s_rest = deal_rest("w_s_rest", ws, "w_s_rest")
-        cand_w = held.tile([P, C], U32, name="cand_w", tag="ws", align_bytes=64)
-        nc.vector.tensor_copy(dealt(cand_w[:]), xw[:].bitcast(U32).indirect(cand_l[:]))
+        nc.vector.tensor_copy(tok_w[:], x_loaded[:].bitcast(U32).indirect(offs_l[:]))
+        w_s_first = deal_first("w_s_first", w_plane)
+        w_s_rest = deal_rest("w_s_rest", w_plane)
+        cand_w = sb("cand_w", [P, C], U32, bytes_of="w_plane")
+        nc.vector.tensor_copy(dealt(cand_w[:]), x_loaded[:].bitcast(U32).indirect(cand_l[:]))
 
-        y_ps = [psum.tile([P, S], F32, name=f"y_ps{t}", tag=f"bank{t}") for t in tiles]
-        last = PACK - 1
+        y_ps = [bank(f"y_ps{t}", t, S) for t in tiles]
         for t in (0, last, 1, 2):
-            rows = slice(t * P, (t + 1) * P)
-            nc.tensor.matmul_mx(out=y_ps[t][:], lhsT=w_w[:, rows].bitcast(FP8X4), lhsT_scale=tile_scales(w_s_first, w_s_rest, t),
-                                rhs=tok_w[:].bitcast(FP8X4), rhs_scale=tok_s[:], start=True, stop=True)
-
-        cand_s_first = deal_first("cand_s_first", cand_s_listed, "cand_s_first")
+            product(y_ps[t], w_w, t, w_s_first[:] if t == 0 else rest_of(w_s_rest, t), tok_w[:], tok_s[:])
+        cand_s_first = deal_first("cand_s_first", cand_s_listed, bytes_of="w_s_first")
 
         y_win = [sb(f"y_win{t}", [P, WIDE], F32) for t in tiles]
-        total = [sb(f"total{t}", [P, S], F32)[:] for t in tiles]
+        total = [sb(f"total{t}", [P, S], F32) for t in tiles]
         lse = [sb(f"lse{t}", [P, S], F32) for t in tiles]
         diff = [sb(f"diff{t}", [P, S], F32) for t in tiles]
+        copied_on_vector = 1
+        negated_on_scalar = range(1, last)
 
         def negate_on_vector(t):
             nc.vector.tensor_scalar(y_win[t][:, :S], y_ps[t][:], -1.0, None, ALU.mult)
@@ -133,17 +163,17 @@ def tile_picked_candlsemix_none_po_kernel(tc, x_words, x_scales, w1_words, w1_sc
         negate_on_vector(last)
         for t in tiles:
             nc.scalar.activation(win[t][:, :S], y_ps[t][:], ACT.Exp)
-            if t != 1:
+            if t != copied_on_vector:
                 nc.scalar.activation(y_win[t][:, S:], y_ps[t][:], ACT.Exp)
         for t in tiles:
-            nc.vector.tensor_tensor(total[t], win[t][:].indirect(n1_l[:]), y_win[t][:, S:], ALU.add)
+            nc.vector.tensor_tensor(total[t][:], win[t][:].indirect(n1_l[:]), y_win[t][:, S:], ALU.add)
             if t == 0:
-                nc.vector.tensor_copy(y_win[1][:, S:], win[1][:, :S])
+                nc.vector.tensor_copy(y_win[copied_on_vector][:, S:], win[copied_on_vector][:, :S])
                 negate_on_vector(0)
         for t in tiles:
-            if t in (1, 2):
+            if t in negated_on_scalar:
                 nc.scalar.activation(y_win[t][:, :S], y_ps[t][:], ACT.Copy, scale=-1.0)
-            nc.scalar.activation(lse[t][:], total[t], ACT.Ln)
+            nc.scalar.activation(lse[t][:], total[t][:], ACT.Ln)
 
         z_rows = sb("z_rows", [P, 2, PACK, HALF], BF16)
         z_quad = [sb(f"z_quad{h}", [P, HALF, PACK], BF16) for h in halves]
@@ -151,80 +181,73 @@ def tile_picked_candlsemix_none_po_kernel(tc, x_words, x_scales, w1_words, w1_sc
         z_s = sb("z_s", [P, S], U8)
         for t in range(last):
             nc.vector.tensor_tensor(diff[t][:], y_win[t][:].indirect(n2_l[:]), lse[t][:], ALU.add)
-            nc.scalar.activation(z_rows[:, :, t, :], diff[t][:].rearrange("p (h j) -> p h j", h=2), ACT.Copy, scale=gain[:, t : t + 1])
+            by_half = diff[t][:].rearrange("p (h j) -> p h j", h=2)
+            nc.scalar.activation(z_rows[:, :, t, :], by_half, ACT.Copy, scale=gain[:, t : t + 1])
         for h in halves:
-            nc.vector.tensor_tensor(diff[last][:, half_cols[h]], y_win[last][:].indirect(entries(n2_l, h * HALF, HALF)), lse[last][:, half_cols[h]], ALU.add)
-            nc.vector.tensor_scalar(z_rows[:, h, last, :], diff[last][:, half_cols[h]], gain[:, last : last + 1], None, ALU.mult)
+            cols = half_cols[h]
+            nc.vector.tensor_tensor(diff[last][:, cols], y_win[last][:].indirect(half_of(n2_l, h)), lse[last][:, cols], ALU.add)
+            nc.vector.tensor_scalar(z_rows[:, h, last, :], diff[last][:, cols], gain[:, last : last + 1], None, ALU.mult)
         interleave(nc.scalar.copy, z_quad[0][:], z_rows[:, 0])
         interleave(nc.vector.tensor_copy, z_quad[1][:], z_rows[:, 1])
 
-        def score(t, scale, bank, cols):
-            rows = slice(t * P, (t + 1) * P)
-            nc.tensor.matmul_mx(out=bank[:], lhsT=cand_w[:, rows].bitcast(FP8X4), lhsT_scale=scale,
-                                rhs=z_w[:, cols].bitcast(FP8X4), rhs_scale=z_s[:, cols], start=True, stop=True)
-            nc.scalar.activation(win[t][:, cols], bank[:], ACT.Copy, scale=-0.0625)
+        def score(t, scales, dst, cols):
+            product(dst, cand_w, t, scales, z_w[:, cols], z_s[:, cols])
+            nc.scalar.activation(win[t][:, cols], dst[:], ACT.Copy, scale=-SCORE_SCALE)
 
-        s_parts = {}
         for h in halves:
-            nc.vector.quantize_mx(out=z_w[:, half_cols[h]].bitcast(FP8X4), scales=z_s[:, half_cols[h]], in_=z_quad[h][:].rearrange("p j t -> p (j t)"))
-            s_parts[0, h] = psum.tile([P, HALF], F32, name=f"s_ps0_{h}", tag=f"bank{4 + h}")
-            score(0, cand_s_first[:], s_parts[0, h], half_cols[h])
-        cand_s_rest = deal_rest("cand_s_rest", cand_s_listed, "z_quad1")
+            quantize(z_w[:, half_cols[h]], z_s[:, half_cols[h]], z_quad[h][:])
+            score(0, cand_s_first[:], bank(f"s_ps0_{h}", PACK + h, HALF), half_cols[h])
+        cand_s_rest = deal_rest("cand_s_rest", cand_s_listed, bytes_of="z_quad1")
+        s_banks = {1: 6, 2: 7, 3: 0}
         s_ps = {}
         pos_s = [sb(f"pos_s{t}", [P, S], F32) for t in range(TURNED)]
         for t in range(1, PACK):
-            s_ps[t] = psum.tile([P, S], F32, name=f"s_ps{t}", tag=f"bank{(5 + t) % 8}")
+            s_ps[t] = bank(f"s_ps{t}", s_banks[t], S)
             if t <= TURNED:
                 nc.scalar.activation(pos_s[t - 1][:], win[t - 1][:, :S], ACT.Copy, scale=-1.0)
-            score(t, cand_s_rest[:, (t - 1) * P : t * P], s_ps[t], slice(0, S))
+            score(t, rest_of(cand_s_rest, t), s_ps[t], whole)
 
         out_rows = out_0.rearrange("(p t) j -> p t j", t=PACK)
         o_w = sb("o_w", [P, S], U32)
         o_s = sb("o_s", [P, S], U8)
-        res = [sb(f"res{u}", [P, 2, S], F32) for u in range(2)]
+        res = [sb(f"res{u}", [P, 2, S], F32) for u in range(PACK // 2)]
         res_quad = sb("res_quad", [P, S, PACK], BF16)
-        whole = slice(0, S)
         blocks = [slice(b * P, (b + 1) * P) for b in range(S // P)]
 
-        def store(queue, t, cols):
-            queue.dma_start(out_rows[:, t, cols], res[t // 2][:, t % 2, cols])
+        def result(t, cols):
+            return res[t // 2][:, t % 2, cols]
 
         def round_pair(copy, u, cols):
             interleave(copy, res_quad[:, cols, 2 * u : 2 * u + 2], res[u][:, :, cols])
 
-        def planes(cols):
-            nc.vector.quantize_mx(out=o_w[:, cols].bitcast(FP8X4), scales=o_s[:, cols], in_=res_quad[:, cols, :].rearrange("p j t -> p (j t)"))
-            nc.sync.dma_start(as_words(out_1)[:, cols], o_w[:, cols].bitcast(I32))
-
         turned = [sb(f"turned{t}", [P, S], F32) for t in range(TURNED)]
-
-        def turn_back(t):
-            back = psum.tile([P, S], F32, name=f"back{t}", tag="bank2")
-            for block in blocks:
-                nc.tensor.transpose(back[:, block], turned[t][:, block], ident[:])
-            nc.scalar.copy(res[t // 2][:, t % 2, :], back[:])
-            store(nc.scalar, t, whole)
-
         for t in range(TURNED):
             neg4 = sb(f"neg4_{t}", [P, S], F32)
             below3 = sb(f"below3_{t}", [P, S], F32)
             gap = sb(f"gap{t}", [P, S], F32)
-            rise = held.tile([P, S], F32, name=f"rise{t}", tag="rise", align_bytes=64)
+            rise = sb(f"rise{t}", [P, S], F32)
+            over = sb(f"over{t}", [P, S], F32)
             drop = sb(f"drop{t}", [P, S], F32)
             nc.vector.tensor_copy(neg4[:], win[t][:].indirect(n4_l[:]))
             nc.vector.tensor_tensor(below3[:], win[t][:].indirect(n3_l[:]), pos_s[t][:], ALU.add)
             nc.scalar.activation(rise[:], below3[:], ACT.Relu, scale=-1.0)
             nc.vector.tensor_tensor(gap[:], win[t][:].indirect(n5_l[:]), neg4[:], ALU.subtract)
-            nc.vector.tensor_scalar(drop[:], gap[:], 0.0, None, ALU.min)
-            if t > 0:
-                turn_back(t - 1)
-            summed = psum.tile([P, S], F32, name=f"summed{t}", tag="bank1")
+            nc.scalar.activation(over[:], gap[:], ACT.Relu, scale=-1.0)
+            nc.scalar.activation(drop[:], over[:], ACT.Copy, scale=-1.0)
+            summed = bank(f"summed{t}", 1 + t, S)
             terms = (pos_s[t], neg4, rise, drop)
             for block in blocks:
                 for i, term in enumerate(terms):
-                    nc.tensor.matmul(summed[:, block], term[:, block], ident[:], is_transpose=True, start=i == 0, stop=i == len(terms) - 1)
+                    nc.tensor.matmul(
+                        summed[:, block], term[:, block], ident[:], is_transpose=True, start=i == 0, stop=i == len(terms) - 1
+                    )
             nc.scalar.copy(turned[t][:], summed[:])
-        turn_back(TURNED - 1)
+        for t in range(TURNED):
+            back = bank(f"back{t}", 1 + TURNED + t, S)
+            for block in blocks:
+                nc.tensor.transpose(back[:, block], turned[t][:, block], ident[:])
+            nc.scalar.copy(result(t, whole), back[:])
+            nc.scalar.dma_start(out_rows[:, t, whole], result(t, whole))
         round_pair(nc.scalar.copy, 0, whole)
 
         direct = range(TURNED, PACK)
@@ -233,27 +256,31 @@ def tile_picked_candlsemix_none_po_kernel(tc, x_words, x_scales, w1_words, w1_sc
         less4 = {t: sb(f"less4_{t}", [P, S], F32) for t in direct}
         less5 = {t: sb(f"less5_{t}", [P, S], F32) for t in direct}
 
+        def subtract_from_top(dst, t, offsets, cols):
+            nc.vector.tensor_tensor(dst[t][:, cols], win[t][:].indirect(offsets), neg_top[t][:, cols], ALU.subtract)
+
         def finish(t, cols):
-            nc.vector.tensor_tensor(res[1][:, t % 2, cols], less4[t][:, cols], less5[t][:, cols], ALU.min)
-            store(nc.sync, t, cols)
+            nc.vector.tensor_tensor(result(t, cols), less4[t][:, cols], less5[t][:, cols], ALU.min)
+            nc.sync.dma_start(out_rows[:, t, cols], result(t, cols))
 
         for t in direct:
             nc.vector.tensor_copy(neg3[t][:], win[t][:].indirect(n3_l[:]))
         for t in direct:
-            nc.vector.scalar_tensor_tensor(neg_top[t][:], s_ps[t][:], -0.0625, neg3[t][:], ALU.mult, ALU.min)
-        for lst, less in ((n4_l, less4), (n5_l, less5)):
-            nc.vector.tensor_tensor(less[TURNED][:], win[TURNED][:].indirect(lst[:]), neg_top[TURNED][:], ALU.subtract)
-        nc.vector.tensor_tensor(less4[last][:], win[last][:].indirect(n4_l[:]), neg_top[last][:], ALU.subtract)
+            nc.vector.scalar_tensor_tensor(neg_top[t][:], s_ps[t][:], -SCORE_SCALE, neg3[t][:], ALU.mult, ALU.min)
+        subtract_from_top(less4, TURNED, n4_l[:], whole)
+        subtract_from_top(less5, TURNED, n5_l[:], whole)
+        subtract_from_top(less4, last, n4_l[:], whole)
         finish(TURNED, whole)
         for h in halves:
-            cols = half_cols[h]
-            nc.vector.tensor_tensor(less5[last][:, cols], win[last][:].indirect(entries(n5_l, h * HALF, HALF)), neg_top[last][:, cols], ALU.subtract)
+            subtract_from_top(less5, last, half_of(n5_l, h), half_cols[h])
         for h in halves:
             finish(last, half_cols[h])
         for h in halves:
             round_pair(nc.vector.tensor_copy, 1, half_cols[h])
         for h in halves:
-            planes(half_cols[h])
-        for q in range(4):
+            cols = half_cols[h]
+            quantize(o_w[:, cols], o_s[:, cols], res_quad[:, cols, :])
+            nc.sync.dma_start(as_words(out_1)[:, cols], o_w[:, cols].bitcast(I32))
+        for q in quadrants:
             queue = nc.scalar if q % 2 == 0 else nc.sync
-            queue.dma_start(out_2[0, 4 * q : 4 * q + 4, :].bitcast(I32), o_s[32 * q : 32 * q + 4, :].bitcast(I32))
+            queue.dma_start(scale_rows(out_2, q), live_rows(o_s, q))

from contextlib import ExitStack

import concourse.mybir as mybir
from concourse.masks import make_identity

K, T, S, H, C = 512, 2048, 512, 512, 512
FLOPS = 2 * K * H * S + 2 * K * C * S

F32 = mybir.dt.float32
BF16 = mybir.dt.bfloat16
I32 = mybir.dt.int32
U32 = mybir.dt.uint32
U16 = mybir.dt.uint16
U8 = mybir.dt.uint8
FP8X4 = mybir.dt.float8_e4m3fn_x4
ACT = mybir.ActivationFunctionType
ALU = mybir.AluOpType

P = 128
PACK = 4
QUADRANT = 32
SCALE_ROWS = 4
STRIPE = 16
HALF = S // 2
WIDE = 2 * S
RUN = 4
SCORE_SCALE = 0.0625
TURNED = 2


def tile_picked_candlsemix_none_po_kernel(
    tc, x_words, x_scales, w1_words, w1_scales, gs, offs, n1, n2, cand, n3, n4, n5, out_0, out_1, out_2
):
    nc = tc.nc
    tiles = range(PACK)
    halves = range(2)
    quadrants = range(P // QUADRANT)
    last = PACK - 1
    whole = slice(0, S)
    half_cols = [slice(h * HALF, (h + 1) * HALF) for h in halves]

    with ExitStack() as ctx:
        held = ctx.enter_context(tc.tile_pool(name="held", bufs=1))
        psum = ctx.enter_context(tc.psum_pool(name="psum", bufs=1))

        def sb(name, shape, dtype, bytes_of=None):
            return held.tile(shape, dtype, name=name, tag=bytes_of or name, align_bytes=64)

        def bank(name, number, width):
            return psum.tile([P, width], F32, name=name, tag=f"bank{number}")

        def load_list(name, src):
            lst = held.tile([P, S // STRIPE], U16, name=name)
            nc.sync.dma_start(lst[:], src)
            return lst

        def half_of(lst, h):
            return lst[:, h * HALF // STRIPE : (h + 1) * HALF // STRIPE]

        def live_rows(plane, q):
            return plane[QUADRANT * q : QUADRANT * q + SCALE_ROWS, :].bitcast(I32)

        def scale_rows(dram, q):
            return dram[0, SCALE_ROWS * q : SCALE_ROWS * (q + 1), :].bitcast(I32)

        def load_scales(plane, src):
            for q in quadrants:
                nc.sync.dma_start(live_rows(plane, q), scale_rows(src, q))

        def as_words(dram):
            return dram[0].rearrange("p n t -> p (n t)").bitcast(I32)

        def dealt(ap):
            return ap.rearrange("p (t m) -> p m t", t=PACK)

        def in_order(ap):
            return ap.rearrange("p (m t) -> p m t", t=PACK)

        def deal_first(name, src, bytes_of=None):
            dst = sb(name, [P, P], U8, bytes_of)
            nc.vector.tensor_copy(dst[:], in_order(src[:])[:, :, 0])
            return dst

        def deal_rest(name, src, bytes_of=None):
            dst = sb(name, [P, last * P], U8, bytes_of)
            nc.vector.tensor_copy(dst[:].rearrange("p (t m) -> p m t", t=last), in_order(src[:])[:, :, 1:])
            return dst

        def rest_of(rest, t):
            return rest[:, (t - 1) * P : t * P]

        def product(dst, words, t, scales, moving_words, moving_scales):
            nc.tensor.matmul_mx(
                out=dst[:],
                lhsT=words[:, t * P : (t + 1) * P].bitcast(FP8X4),
                lhsT_scale=scales,
                rhs=moving_words.bitcast(FP8X4),
                rhs_scale=moving_scales,
                start=True,
                stop=True,
            )

        def interleave(copy, dst, src):
            copy(dst.rearrange("p (c i) t -> p c t i", i=RUN), src.rearrange("p t (c i) -> p c t i", i=RUN))

        def quantize(words, scales, quad):
            nc.vector.quantize_mx(out=words.bitcast(FP8X4), scales=scales, in_=quad.rearrange("p j t -> p (j t)"))

        x_plane = sb("x_plane", [P, T], U8)
        w_plane = sb("w_plane", [P, H], U8)
        nc.vector.memset(x_plane[:].bitcast(I32), 0)
        nc.vector.memset(w_plane[:].bitcast(I32), 0)
        offs_l = load_list("offs_l", offs)
        cand_l = load_list("cand_l", cand)
        w_loaded = sb("w_loaded", [P, H], I32)
        nc.sync.dma_start(w_loaded[:], as_words(w1_words))
        load_scales(x_plane, x_scales)
        x_loaded = sb("x_loaded", [P, T], I32)
        nc.sync.dma_start(x_loaded[:], as_words(x_words))
        load_scales(w_plane, w1_scales)
        n1_l = load_list("n1_l", n1)
        gain = sb("gain", [P, PACK], F32)
        nc.sync.dma_start(gain[:], gs.rearrange("(p t) o -> p (t o)", t=PACK))
        n2_l = load_list("n2_l", n2)
        n3_l = load_list("n3_l", n3)
        n4_l = load_list("n4_l", n4)
        n5_l = load_list("n5_l", n5)

        win = [sb(f"win{t}", [P, WIDE], F32) for t in tiles]
        for t in tiles:
            nc.vector.memset(win[t][:, S:], 0.0)
        ident = sb("ident", [P, P], F32)
        make_identity(nc, ident[:])

        tok_s = sb("tok_s", [P, S], U8)
        nc.vector.tensor_copy(tok_s[:], x_plane[:].indirect(offs_l[:]))
        w_w = sb("w_w", [P, H], I32)
        nc.vector.tensor_copy(dealt(w_w[:]), in_order(w_loaded[:]))
        cand_s_listed = sb("cand_s_listed", [P, C], U8)
        nc.vector.tensor_copy(cand_s_listed[:], x_plane[:].indirect(cand_l[:]))
        tok_w = sb("tok_w", [P, S], U32)
        nc.vector.tensor_copy(tok_w[:], x_loaded[:].bitcast(U32).indirect(offs_l[:]))
        w_s_first = deal_first("w_s_first", w_plane)
        w_s_rest = deal_rest("w_s_rest", w_plane)
        cand_w = sb("cand_w", [P, C], U32, bytes_of="w_plane")
        nc.vector.tensor_copy(dealt(cand_w[:]), x_loaded[:].bitcast(U32).indirect(cand_l[:]))

        y_ps = [bank(f"y_ps{t}", t, S) for t in tiles]
        for t in (0, last, 1, 2):
            product(y_ps[t], w_w, t, w_s_first[:] if t == 0 else rest_of(w_s_rest, t), tok_w[:], tok_s[:])
        cand_s_first = deal_first("cand_s_first", cand_s_listed, bytes_of="w_s_first")

        y_win = [sb(f"y_win{t}", [P, WIDE], F32) for t in tiles]
        total = [sb(f"total{t}", [P, S], F32) for t in tiles]
        lse = [sb(f"lse{t}", [P, S], F32) for t in tiles]
        diff = [sb(f"diff{t}", [P, S], F32) for t in tiles]
        copied_on_vector = 1
        negated_on_scalar = range(1, last)

        def negate_on_vector(t):
            nc.vector.tensor_scalar(y_win[t][:, :S], y_ps[t][:], -1.0, None, ALU.mult)

        negate_on_vector(last)
        for t in tiles:
            nc.scalar.activation(win[t][:, :S], y_ps[t][:], ACT.Exp)
            if t != copied_on_vector:
                nc.scalar.activation(y_win[t][:, S:], y_ps[t][:], ACT.Exp)
        for t in tiles:
            nc.vector.tensor_tensor(total[t][:], win[t][:].indirect(n1_l[:]), y_win[t][:, S:], ALU.add)
            if t == 0:
                nc.vector.tensor_copy(y_win[copied_on_vector][:, S:], win[copied_on_vector][:, :S])
                negate_on_vector(0)
        for t in tiles:
            if t in negated_on_scalar:
                nc.scalar.activation(y_win[t][:, :S], y_ps[t][:], ACT.Copy, scale=-1.0)
            nc.scalar.activation(lse[t][:], total[t][:], ACT.Ln)

        z_rows = sb("z_rows", [P, 2, PACK, HALF], BF16)
        z_quad = [sb(f"z_quad{h}", [P, HALF, PACK], BF16) for h in halves]
        z_w = sb("z_w", [P, S], U32)
        z_s = sb("z_s", [P, S], U8)
        for t in range(last):
            nc.vector.tensor_tensor(diff[t][:], y_win[t][:].indirect(n2_l[:]), lse[t][:], ALU.add)
            by_half = diff[t][:].rearrange("p (h j) -> p h j", h=2)
            nc.scalar.activation(z_rows[:, :, t, :], by_half, ACT.Copy, scale=gain[:, t : t + 1])
        for h in halves:
            cols = half_cols[h]
            nc.vector.tensor_tensor(diff[last][:, cols], y_win[last][:].indirect(half_of(n2_l, h)), lse[last][:, cols], ALU.add)
            nc.vector.tensor_scalar(z_rows[:, h, last, :], diff[last][:, cols], gain[:, last : last + 1], None, ALU.mult)
        interleave(nc.scalar.copy, z_quad[0][:], z_rows[:, 0])
        interleave(nc.vector.tensor_copy, z_quad[1][:], z_rows[:, 1])

        def score(t, scales, dst, cols):
            product(dst, cand_w, t, scales, z_w[:, cols], z_s[:, cols])
            nc.scalar.activation(win[t][:, cols], dst[:], ACT.Copy, scale=-SCORE_SCALE)

        for h in halves:
            quantize(z_w[:, half_cols[h]], z_s[:, half_cols[h]], z_quad[h][:])
            score(0, cand_s_first[:], bank(f"s_ps0_{h}", PACK + h, HALF), half_cols[h])
        cand_s_rest = deal_rest("cand_s_rest", cand_s_listed, bytes_of="z_quad1")
        s_banks = {1: 6, 2: 7, 3: 0}
        s_ps = {}
        pos_s = [sb(f"pos_s{t}", [P, S], F32) for t in range(TURNED)]
        for t in range(1, PACK):
            s_ps[t] = bank(f"s_ps{t}", s_banks[t], S)
            if t <= TURNED:
                nc.scalar.activation(pos_s[t - 1][:], win[t - 1][:, :S], ACT.Copy, scale=-1.0)
            score(t, rest_of(cand_s_rest, t), s_ps[t], whole)

        out_rows = out_0.rearrange("(p t) j -> p t j", t=PACK)
        o_w = sb("o_w", [P, S], U32)
        o_s = sb("o_s", [P, S], U8)
        res = [sb(f"res{u}", [P, 2, S], F32) for u in range(PACK // 2)]
        res_quad = sb("res_quad", [P, S, PACK], BF16)
        blocks = [slice(b * P, (b + 1) * P) for b in range(S // P)]

        def result(t, cols):
            return res[t // 2][:, t % 2, cols]

        def round_pair(copy, u, cols):
            interleave(copy, res_quad[:, cols, 2 * u : 2 * u + 2], res[u][:, :, cols])

        turned = [sb(f"turned{t}", [P, S], F32) for t in range(TURNED)]
        for t in range(TURNED):
            neg4 = sb(f"neg4_{t}", [P, S], F32)
            below3 = sb(f"below3_{t}", [P, S], F32)
            gap = sb(f"gap{t}", [P, S], F32)
            rise = sb(f"rise{t}", [P, S], F32)
            over = sb(f"over{t}", [P, S], F32)
            drop = sb(f"drop{t}", [P, S], F32)
            nc.vector.tensor_copy(neg4[:], win[t][:].indirect(n4_l[:]))
            nc.vector.tensor_tensor(below3[:], win[t][:].indirect(n3_l[:]), pos_s[t][:], ALU.add)
            nc.scalar.activation(rise[:], below3[:], ACT.Relu, scale=-1.0)
            nc.vector.tensor_tensor(gap[:], win[t][:].indirect(n5_l[:]), neg4[:], ALU.subtract)
            nc.scalar.activation(over[:], gap[:], ACT.Relu, scale=-1.0)
            nc.scalar.activation(drop[:], over[:], ACT.Copy, scale=-1.0)
            summed = bank(f"summed{t}", 1 + t, S)
            terms = (pos_s[t], neg4, rise, drop)
            for block in blocks:
                for i, term in enumerate(terms):
                    nc.tensor.matmul(
                        summed[:, block], term[:, block], ident[:], is_transpose=True, start=i == 0, stop=i == len(terms) - 1
                    )
            nc.scalar.copy(turned[t][:], summed[:])
        for t in range(TURNED):
            back = bank(f"back{t}", 1 + TURNED + t, S)
            for block in blocks:
                nc.tensor.transpose(back[:, block], turned[t][:, block], ident[:])
            nc.scalar.copy(result(t, whole), back[:])
            nc.scalar.dma_start(out_rows[:, t, whole], result(t, whole))
        round_pair(nc.scalar.copy, 0, whole)

        direct = range(TURNED, PACK)
        neg3 = {t: sb(f"neg3_{t}", [P, S], F32) for t in direct}
        neg_top = {t: sb(f"neg_top{t}", [P, S], F32) for t in direct}
        less4 = {t: sb(f"less4_{t}", [P, S], F32) for t in direct}
        less5 = {t: sb(f"less5_{t}", [P, S], F32) for t in direct}

        def subtract_from_top(dst, t, offsets, cols):
            nc.vector.tensor_tensor(dst[t][:, cols], win[t][:].indirect(offsets), neg_top[t][:, cols], ALU.subtract)

        def finish(t, cols):
            nc.vector.tensor_tensor(result(t, cols), less4[t][:, cols], less5[t][:, cols], ALU.min)
            nc.sync.dma_start(out_rows[:, t, cols], result(t, cols))

        for t in direct:
            nc.vector.tensor_copy(neg3[t][:], win[t][:].indirect(n3_l[:]))
        for t in direct:
            nc.vector.scalar_tensor_tensor(neg_top[t][:], s_ps[t][:], -SCORE_SCALE, neg3[t][:], ALU.mult, ALU.min)
        subtract_from_top(less4, TURNED, n4_l[:], whole)
        subtract_from_top(less5, TURNED, n5_l[:], whole)
        subtract_from_top(less4, last, n4_l[:], whole)
        finish(TURNED, whole)
        for h in halves:
            subtract_from_top(less5, last, half_of(n5_l, h), half_cols[h])
        for h in halves:
            finish(last, half_cols[h])
        for h in halves:
            round_pair(nc.vector.tensor_copy, 1, half_cols[h])
        for h in halves:
            cols = half_cols[h]
            quantize(o_w[:, cols], o_s[:, cols], res_quad[:, cols, :])
            nc.sync.dma_start(as_words(out_1)[:, cols], o_w[:, cols].bitcast(I32))
        for q in quadrants:
            queue = nc.scalar if q % 2 == 0 else nc.sync
            queue.dma_start(scale_rows(out_2, q), live_rows(o_s, q))
